import numpy as np
import ml_dtypes


def mxq(x, axis, fmt="e4m3"):
    dtype, down = {"e4m3": (ml_dtypes.float8_e4m3fn, 7), "e5m2": (ml_dtypes.float8_e5m2, 14)}[fmt]
    v = np.moveaxis(np.asarray(x, np.float32).astype(ml_dtypes.bfloat16).astype(np.float64), axis, -1)
    blocks = v.reshape(v.shape[:-1] + (-1, 32))
    amax = np.abs(blocks).max(-1, keepdims=True)
    byte = np.maximum(np.where(amax > 0, np.frexp(amax)[1] - 1 + 127, 0) - down, 1)
    scale = np.exp2(byte - 127.0)
    codes = (blocks / scale).astype(np.float32).astype(dtype).astype(np.float64)
    return np.moveaxis((codes * scale).reshape(v.shape), -1, axis)


WIDE = False


def mx_kscale(k):
    if not WIDE:
        return np.ones(k)
    levels = np.array([10, -10, 5, -5, 0])
    if k % 512:
        return np.exp2(np.random.permutation(np.resize(levels, k // 32))).repeat(32)
    a = np.empty((k // 512, 16))
    for p in range(k // 512):
        a[p, :8] = np.random.permutation(np.resize(levels, 8))
        for g in range(8):
            far = levels[np.abs(levels - a[p, g]) >= 10]
            a[p, g + 8] = far[np.random.randint(len(far))]
    return np.exp2(a.ravel()).repeat(32)


def f64(x):
    return np.asarray(x).astype(np.float64)


def striped(idx):
    return np.tile(idx.reshape(-1, 16).T, (8, 1)).astype(np.uint16)


def unstriped(offs):
    return offs[:16].T.reshape(-1).astype(np.int64)


def striped8(idx):
    return np.concatenate([x.reshape(-1, 16).T for x in idx]).astype(np.uint16)


def runs(offs, k):
    lists = np.stack([offs[16 * r : 16 * r + 16].T.reshape(-1) for r in range(8)]).astype(np.int64)
    return lists[np.arange(k) % 512 // 64]


def pack_weight(w):
    k, n = w.shape
    w = f64(np.asarray(w, np.float32).astype(ml_dtypes.bfloat16)).reshape(k // 32, 32, n)
    amax = np.abs(w).max(1)
    byte = np.clip(np.where(amax > 0, np.frexp(amax)[1] - 1 + 127 - 7, 1), 1, 254)
    scaled = (w * np.exp2(127.0 - byte)[:, None, :]).reshape(k, n).astype(np.float32)
    words = np.ascontiguousarray(scaled.reshape(k // 512, 128, 4, n).transpose(0, 1, 3, 2)).astype(ml_dtypes.float8_e4m3fn).view(np.uint8)
    return words, np.ascontiguousarray(byte.astype(np.uint8).reshape(k // 512, 16, n))


def unpack_weight(words, scales):
    g, p, n, _ = words.shape
    vals = np.ascontiguousarray(words).view(ml_dtypes.float8_e4m3fn).astype(np.float64) * np.repeat(np.exp2(scales.astype(np.float64) - 127.0), 8, axis=1)[..., None]
    return vals.transpose(0, 1, 3, 2).reshape(g * 512, n)


E2M1 = np.array([0.0, 0.5, 1.0, 1.5, 2.0, 3.0, 4.0, 6.0, -0.0, -0.5, -1.0, -1.5, -2.0, -3.0, -4.0, -6.0])


def pack_fp4(w):
    k, n = w.shape
    w = f64(np.asarray(w, np.float32).astype(ml_dtypes.bfloat16)).reshape(k // 32, 32, n)
    amax = np.abs(w).max(1)
    mant, ex = np.frexp(amax / 6.0)
    byte = np.clip(np.where(amax > 0, np.where(mant > 0.5, ex, ex - 1) + 127, 1), 1, 254)
    scaled = (w * np.exp2(127.0 - byte)[:, None, :]).reshape(k, n).astype(np.float32)
    c = np.ascontiguousarray(scaled.reshape(k // 512, 128, 4, n).transpose(0, 1, 3, 2)).astype(ml_dtypes.float4_e2m1fn).view(np.uint8) & 0xF
    words = (c[..., 0::2] | (c[..., 1::2] << 4)).reshape(k // 512, 128, 2 * n)
    return np.ascontiguousarray(words), np.ascontiguousarray(byte.astype(np.uint8).reshape(k // 512, 16, n))


def unpack_fp4(words, scales):
    g, _, n = scales.shape
    words = np.ascontiguousarray(words).reshape(g, 128, n, 2)
    nib = np.empty((g, 128, n, 4), np.uint8)
    nib[..., 0::2] = words & 0xF
    nib[..., 1::2] = words >> 4
    vals = E2M1[nib] * np.repeat(np.exp2(scales.astype(np.float64) - 127.0), 8, axis=1)[..., None]
    return vals.transpose(0, 1, 3, 2).reshape(g * 512, n)


def planes(y):
    n, m = y.shape
    v = y.astype(np.float32).astype(ml_dtypes.bfloat16).astype(np.float64).reshape(n // 32, 32, m)
    top = np.abs(v).max(1)
    byte = np.clip(np.where(top > 0, np.frexp(top)[1] - 1 + 127 - 7, 1), 1, 254)
    codes = (v * np.exp2(127.0 - byte)[:, None, :]).reshape(n, m).astype(np.float32).astype(ml_dtypes.float8_e4m3fn).view(np.uint8)
    words = codes.reshape(n // 512, 128, 4, m).transpose(0, 1, 3, 2)
    return np.ascontiguousarray(words), np.ascontiguousarray(byte.astype(np.uint8).reshape(n // 512, 16, m))


K, T, S, V, N, H, U = 512, 2048, 1024, 512, 512, 512, 1024


def setup_inputs():
    n = np.random.standard_normal
    s = mx_kscale(K)[:, None]
    u = mx_kscale(H)
    packed_xT = pack_weight(n((K, T)) * s)
    packed_w3 = pack_fp4(n((H, N)) / np.sqrt(H) / u[:, None])
    return {
        "x_words": packed_xT[0],
        "x_scales": packed_xT[1],
        "w1": (n((K, H)) / np.sqrt(K) / s * u).astype(np.float32),
        "w2": (n((H, H)) / np.sqrt(H) / u[:, None] * u).astype(np.float32),
        "mem": (n((H, U)) * u[:, None]).astype(np.float32),
        "w3_words": packed_w3[0],
        "w3_scales": packed_w3[1],
        "res": n((N, U)).astype(np.float32),
        "offs": striped(np.random.permutation(T)[:S]),
        "n1": striped8(np.stack([np.random.permutation(S) for _ in range(8)])),
        "n2": striped8(np.stack([np.random.permutation(U)[:V] for _ in range(8)])),
        "n3": striped8(np.stack([np.random.permutation(U) for _ in range(8)])),
    }


def reference(x_words, x_scales, w1, w2, mem, w3_words, w3_scales, res, offs, n1, n2, n3):
    xq = unpack_weight(x_words, x_scales)[:, unstriped(offs)]
    y = mxq(f64(w1), 0, "e4m3").T @ xq
    ln = y[np.arange(H)[:, None], runs(n1, H)]
    z = ln.reshape(H, V, 2).max(axis=2)
    h = mxq(f64(w2), 0, "e4m3").T @ mxq(z, 0, "e4m3")
    pg = f64(mem).copy()
    pg[np.arange(H)[:, None], runs(n2, H)] = h
    z2 = pg - (0.5 * (pg[np.arange(H)[:, None], runs(n3, H)]))
    out_0 = f64(res) + (unpack_fp4(w3_words, w3_scales).T @ mxq(z2, 0, "e4m3"))
    return (out_0,) + planes(out_0)

@@ -1,0 +1,249 @@
+from contextlib import ExitStack
+
+import concourse.mybir as mybir
+
+K, T, S, V, N, H, U = 512, 2048, 1024, 512, 512, 512, 1024
+FLOPS = 2 * K * H * S + 2 * H * H * V + 2 * H * N * U
+
+F32 = mybir.dt.float32
+BF16 = mybir.dt.bfloat16
+I32 = mybir.dt.int32
+U32 = mybir.dt.uint32
+U16 = mybir.dt.uint16
+U8 = mybir.dt.uint8
+FP8X4 = mybir.dt.float8_e4m3fn_x4
+FP4X4 = mybir.dt.float4_e2m1fn_x4
+ALU = mybir.AluOpType
+COPY = mybir.ActivationFunctionType.Copy
+
+P = 128
+PACK = 4
+LIST_ROWS = 16
+BANK = 512
+PIECE = 256
+RUN = 4
+
+
+def entries(list_tile, first, count):
+    return list_tile[:, first // LIST_ROWS : (first + count) // LIST_ROWS]
+
+
+def load_scale_rows(engine, tile, rows):
+    for quad in range(4):
+        engine.dma_start(out=tile[32 * quad : 32 * quad + 4, :].bitcast(I32), in_=rows[4 * quad : 4 * quad + 4, :].bitcast(I32))
+
+
+def woven(tile):
+    return tile.rearrange("p (c i t) -> p c t i", i=RUN, t=PACK)
+
+
+def planar(tile):
+    return tile.rearrange("p t (c i) -> p c t i", i=RUN)
+
+
+def tile_picked_deeppoolpagem_none_po_kernel(
+    tc, x_words, x_scales, w1, w2, mem, w3_words, w3_scales, res, offs, n1, n2, n3, out_0, out_1, out_2
+):
+    nc = tc.nc
+    with ExitStack() as ctx:
+        keep = ctx.enter_context(tc.tile_pool(name="keep", bufs=1))
+        ring = ctx.enter_context(tc.tile_pool(name="ring", bufs=2))
+        psum = ctx.enter_context(tc.psum_pool(name="psum", bufs=8))
+
+        def held(shape, dtype, name):
+            return keep.tile(shape, dtype, name=name, align_bytes=64)
+
+        offs_sb = held([P, S // LIST_ROWS], U16, "offs_sb")
+        n1_sb = held([P, S // LIST_ROWS], U16, "n1_sb")
+        n2_sb = held([P, V // LIST_ROWS], U16, "n2_sb")
+        n3_sb = held([P, U // LIST_ROWS], U16, "n3_sb")
+        x_words_sb = held([P, T], U32, "x_words_sb")
+        x_scales_sb = held([P, T], U8, "x_scales_sb")
+        w3_words_sb = held([P, 2 * N], U8, "w3_words_sb")
+        w3_scales_sb = held([P, N], U8, "w3_scales_sb")
+        w1_raw = [held([P, PACK, H // 2], F32, "w1_raw%d" % c) for c in range(2)]
+        w2_raw = held([P, PACK, H], F32, "w2_raw")
+        page = [held([P, U], F32, "page%d" % t) for t in range(PACK)]
+        res_sb = held([P, PACK, U], F32, "res_sb")
+
+        nc.gpsimd.memset(x_scales_sb[:].bitcast(I32), 0)
+        nc.gpsimd.memset(w3_scales_sb[:].bitcast(I32), 0)
+        load_scale_rows(nc.scalar, x_scales_sb, x_scales[0])
+        nc.sync.dma_start(offs_sb[:], offs)
+        nc.sync.dma_start(out=x_words_sb[:].bitcast(I32), in_=x_words[0].rearrange("p n t -> p (n t)").bitcast(I32))
+        w1_rows = w1.rearrange("(p j) c -> p j c", j=PACK)
+        for c in range(2):
+            nc.sync.dma_start(out=w1_raw[c][:], in_=w1_rows[:, :, c * (H // 2) : (c + 1) * (H // 2)])
+        nc.sync.dma_start(out=w3_words_sb[:].bitcast(I32), in_=w3_words[0].bitcast(I32))
+        load_scale_rows(nc.sync, w3_scales_sb, w3_scales[0])
+        nc.sync.dma_start(n1_sb[:], n1)
+        mem_rows = mem.rearrange("(p t) w -> p t w", t=PACK)
+        for t in range(2):
+            nc.sync.dma_start(out=page[t][:], in_=mem_rows[:, t, :])
+        nc.sync.dma_start(out=w2_raw[:], in_=w2.rearrange("(p j) c -> p j c", j=PACK))
+        nc.sync.dma_start(n2_sb[:], n2)
+        nc.sync.dma_start(n3_sb[:], n3)
+        for t in range(2, PACK):
+            nc.sync.dma_start(out=page[t][:], in_=mem_rows[:, t, :])
+        nc.sync.dma_start(out=res_sb[:], in_=res.rearrange("(p t) w -> p t w", t=PACK))
+
+        x_pick_scales = held([P, S], U8, "x_pick_scales")
+        x_pick_words = held([P, S], U32, "x_pick_words")
+        nc.vector.tensor_copy(x_pick_scales[:], x_scales_sb[:].indirect(offs_sb[:]))
+        nc.vector.tensor_copy(x_pick_words[:], x_words_sb[:].indirect(offs_sb[:]))
+
+        def deal_weight(dealt, raw, first_m):
+            count = raw.shape[2] // PACK
+            nc.scalar.copy(
+                out=dealt[:].rearrange("p (t m j) -> p m j t", t=PACK, j=PACK)[:, first_m : first_m + count],
+                in_=raw.rearrange("p j (m t) -> p m j t", t=PACK),
+            )
+
+        def quantize(words, scales, values):
+            nc.vector.quantize_mx(out=words.bitcast(FP8X4), scales=scales, in_=values)
+
+        w1_dealt = keep.tile([P, PACK * H], BF16, tag="dealt", name="w1_dealt", align_bytes=64)
+        w1_words = held([P, H], U32, "w1_words")
+        w1_scales = held([P, H], U8, "w1_scales")
+        for c in range(2):
+            deal_weight(w1_dealt, w1_raw[c][:], c * (P // 2))
+        for c in range(2):
+            cols = slice(c * (H // 2), (c + 1) * (H // 2))
+            quantize(w1_words[:, cols], w1_scales[:, cols], w1_dealt[:, c * 2 * H : (c + 1) * 2 * H])
+
+        y = [held([P, S], F32, "y%d" % t) for t in range(PACK)]
+        for t in range(PACK):
+            rows = slice(t * P, (t + 1) * P)
+            for half in range(S // BANK):
+                cols = slice(half * BANK, (half + 1) * BANK)
+                bank = psum.tile([P, BANK], F32, tag="bank", name="y_bank")
+                nc.tensor.matmul_mx(
+                    out=bank[:],
+                    lhsT=w1_words[:, rows].bitcast(FP8X4),
+                    lhsT_scale=w1_scales[:, rows],
+                    rhs=x_pick_words[:, cols].bitcast(FP8X4),
+                    rhs_scale=x_pick_scales[:, cols],
+                    start=True,
+                    stop=True,
+                )
+                if t == 0 and half == 1:
+                    nc.vector.tensor_copy(out=y[t][:, cols], in_=bank[:])
+                else:
+                    nc.scalar.copy(out=y[t][:, cols], in_=bank[:])
+
+        w3_dealt_words = keep.tile([P, PACK, 2 * P], U8, tag="dealt", name="w3_dealt_words", align_bytes=64)
+        w3_dealt_scales = held([P, PACK, P], U8, "w3_dealt_scales")
+        nc.vector.tensor_copy(
+            out=w3_dealt_words[:].rearrange("p t (m b) -> p t m b", b=2),
+            in_=w3_words_sb[:].rearrange("p (m t b) -> p t m b", t=PACK, b=2),
+        )
+        nc.vector.tensor_copy(out=w3_dealt_scales[:], in_=w3_scales_sb[:].rearrange("p (m t) -> p t m", t=PACK))
+
+        w2_dealt = held([P, PACK * H], BF16, "w2_dealt")
+        w2_words = held([P, H], U32, "w2_words")
+        w2_scales = held([P, H], U8, "w2_scales")
+        deal_weight(w2_dealt, w2_raw[:], 0)
+        quantize(w2_words[:], w2_scales[:], w2_dealt[:])
+
+        def product(lhs_words, lhs_scales, words, scales):
+            width = words.shape[1]
+            share = BANK // width
+            banks = []
+            for first in range(0, PACK, share):
+                bank = psum.tile([P, share, width], F32, tag="bank", name="shared_bank")
+                for i in range(share):
+                    t = first + i
+                    nc.tensor.matmul_mx(
+                        out=bank[:, i, :], lhsT=lhs_words(t), lhsT_scale=lhs_scales(t), rhs=words.bitcast(FP8X4), rhs_scale=scales, start=True, stop=True
+                    )
+                banks.append((slice(first, first + share), bank))
+            return banks
+
+        z_words = held([P, V], U32, "z_words")
+        z_scales = held([P, V], U8, "z_scales")
+        h = []
+        for half in range(V // PIECE):
+            lined = keep.tile([P, PACK, 2 * PIECE], F32, tag="lined", name="lined", align_bytes=64)
+            for t in range(PACK):
+                nc.vector.tensor_copy(lined[:, t, :], y[t][:].indirect(entries(n1_sb, half * 2 * PIECE, 2 * PIECE)))
+            z = ring.tile([P, PACK * PIECE], BF16, tag="z", name="z", align_bytes=64)
+            pairs = lined[:].rearrange("p t (c i e) -> p c t i e", i=RUN, e=2)
+            nc.vector.tensor_tensor(woven(z[:]), pairs[:, :, :, :, 0], pairs[:, :, :, :, 1], ALU.max)
+            cols = slice(half * PIECE, (half + 1) * PIECE)
+            quantize(z_words[:, cols], z_scales[:, cols], z[:])
+            banks = product(
+                lambda t: w2_words[:, t * P : (t + 1) * P].bitcast(FP8X4),
+                lambda t: w2_scales[:, t * P : (t + 1) * P],
+                z_words[:, cols],
+                z_scales[:, cols],
+            )
+            h_half = ring.tile([P, PACK, PIECE], F32, tag="h", name="h_half", align_bytes=64)
+            for rows, bank in banks:
+                nc.scalar.copy(out=h_half[:, rows, :], in_=bank[:])
+            h.append(h_half)
+
+        for half in range(V // PIECE):
+            for t in range(PACK):
+                nc.vector.tensor_copy(page[t][:].indirect(entries(n2_sb, half * PIECE, PIECE)), h[half][:, t, :])
+
+        fetches = [(0, 2 * PIECE), (2 * PIECE, PIECE), (3 * PIECE, PIECE)]
+        doubled = [held([P, PACK, width], F32, "doubled%d" % first) for first, width in fetches]
+        mixed = [held([P, PACK, width], F32, "mixed%d" % first) for first, width in fetches]
+        for f, (first, width) in enumerate(fetches):
+            for t in range(PACK):
+                nc.scalar.activation(doubled[f][:, t, :], page[t][:, first : first + width], COPY, scale=2.0)
+        for f, (first, width) in enumerate(fetches):
+            for t in range(PACK):
+                nc.vector.tensor_tensor(mixed[f][:, t, :], page[t][:].indirect(entries(n3_sb, first, width)), doubled[f][:, t, :], ALU.subtract)
+
+        units = []
+        for f, (first, width) in enumerate(fetches):
+            step = PIECE if f < len(fetches) - 1 else PIECE // 2
+            for start in range(0, width, step):
+                units.append((slice(first + start, first + start + step), mixed[f][:, :, start : start + step]))
+
+        z2_words = held([P, U], U32, "z2_words")
+        z2_scales = held([P, U], U8, "z2_scales")
+        out_words = held([P, U], U32, "out_words")
+        out_scales = held([P, U], U8, "out_scales")
+        out_rows = out_0.rearrange("(p t) w -> p t w", t=PACK)
+        out_1_words = out_1[0].rearrange("p n t -> p (n t)").bitcast(I32)
+        sums = {}
+        results = {}
+
+        def multiply(u):
+            cols, source = units[u]
+            z2 = held([P, PACK * source.shape[2]], BF16, "z2_%d" % u)
+            nc.scalar.activation(woven(z2[:]), planar(source), COPY, scale=-0.5)
+            quantize(z2_words[:, cols], z2_scales[:, cols], z2[:])
+            sums[u] = product(
+                lambda t: w3_dealt_words[:, t, :].bitcast(FP4X4),
+                lambda t: w3_dealt_scales[:, t, :],
+                z2_words[:, cols],
+                z2_scales[:, cols],
+            )
+
+        def add_residual(u):
+            cols, source = units[u]
+            results[u] = held([P, PACK, source.shape[2]], F32, "result%d" % u)
+            for rows, bank in sums[u]:
+                nc.vector.tensor_tensor(results[u][:, rows, :], bank[:], res_sb[:, rows, cols], ALU.add)
+            nc.sync.dma_start(out=out_rows[:, :, cols], in_=results[u][:])
+
+        def hand_on(u):
+            cols, source = units[u]
+            rounded = held([P, PACK * source.shape[2]], BF16, "rounded%d" % u)
+            if u == len(units) - 1:
+                nc.vector.tensor_copy(out=woven(rounded[:]), in_=planar(results[u][:]))
+            else:
+                nc.scalar.copy(out=woven(rounded[:]), in_=planar(results[u][:]))
+            quantize(out_words[:, cols], out_scales[:, cols], rounded[:])
+            nc.sync.dma_start(out=out_1_words[:, cols], in_=out_words[:, cols].bitcast(I32))
+
+        for step in range(len(units) + 2):
+            for lag, stage in enumerate((multiply, add_residual, hand_on)):
+                if 0 <= step - lag < len(units):
+                    stage(step - lag)
+        for quad in range(4):
+            engine = nc.sync if quad % 2 else nc.scalar
+            engine.dma_start(out=out_2[0][4 * quad : 4 * quad + 4, :].bitcast(I32), in_=out_scales[32 * quad : 32 * quad + 4, :].bitcast(I32))

@@ -66,14 +66,14 @@ def tile_picked_deeppoolpagem_none_po_kernel(
         page = [held([P, U], F32, "page%d" % t) for t in range(PACK)]
         res_sb = held([P, PACK, U], F32, "res_sb")
 
-        nc.gpsimd.memset(x_scales_sb[:].bitcast(I32), 0)
+        nc.vector.memset(x_scales_sb[:].bitcast(I32), 0)
         nc.gpsimd.memset(w3_scales_sb[:].bitcast(I32), 0)
-        load_scale_rows(nc.scalar, x_scales_sb, x_scales[0])
         nc.sync.dma_start(offs_sb[:], offs)
-        nc.sync.dma_start(out=x_words_sb[:].bitcast(I32), in_=x_words[0].rearrange("p n t -> p (n t)").bitcast(I32))
         w1_rows = w1.rearrange("(p j) c -> p j c", j=PACK)
-        for c in range(2):
-            nc.sync.dma_start(out=w1_raw[c][:], in_=w1_rows[:, :, c * (H // 2) : (c + 1) * (H // 2)])
+        nc.sync.dma_start(out=w1_raw[0][:], in_=w1_rows[:, :, : H // 2])
+        load_scale_rows(nc.sync, x_scales_sb, x_scales[0])
+        nc.sync.dma_start(out=x_words_sb[:].bitcast(I32), in_=x_words[0].rearrange("p n t -> p (n t)").bitcast(I32))
+        nc.sync.dma_start(out=w1_raw[1][:], in_=w1_rows[:, :, H // 2 :])
         nc.sync.dma_start(out=w3_words_sb[:].bitcast(I32), in_=w3_words[0].bitcast(I32))
         load_scale_rows(nc.sync, w3_scales_sb, w3_scales[0])
         nc.sync.dma_start(n1_sb[:], n1)
@@ -161,46 +161,60 @@ def tile_picked_deeppoolpagem_none_po_kernel(
 
         z_words = held([P, V], U32, "z_words")
         z_scales = held([P, V], U8, "z_scales")
-        h = []
-        for half in range(V // PIECE):
-            lined = keep.tile([P, PACK, 2 * PIECE], F32, tag="lined", name="lined", align_bytes=64)
-            for t in range(PACK):
-                nc.vector.tensor_copy(lined[:, t, :], y[t][:].indirect(entries(n1_sb, half * 2 * PIECE, 2 * PIECE)))
-            z = ring.tile([P, PACK * PIECE], BF16, tag="z", name="z", align_bytes=64)
-            pairs = lined[:].rearrange("p t (c i e) -> p c t i e", i=RUN, e=2)
-            nc.vector.tensor_tensor(woven(z[:]), pairs[:, :, :, :, 0], pairs[:, :, :, :, 1], ALU.max)
+        halves = V // PIECE
+        lined = held([P, PACK + halves - 1, 2 * PIECE], F32, "lined")
+        z = [held([P, PACK * PIECE], BF16, "z%d" % half) for half in range(halves)]
+        h = [held([P, PACK, PIECE], F32, "h%d" % half) for half in range(halves)]
+
+        def line_up(half, t):
+            nc.vector.tensor_copy(lined[:, half + t, :], y[t][:].indirect(entries(n1_sb, half * 2 * PIECE, 2 * PIECE)))
+
+        def pool(half):
+            pairs = lined[:, half : half + PACK, :].rearrange("p t (c i e) -> p c t i e", i=RUN, e=2)
+            nc.vector.tensor_tensor(woven(z[half][:]), pairs[:, :, :, :, 0], pairs[:, :, :, :, 1], ALU.max)
+
+        def project(half):
             cols = slice(half * PIECE, (half + 1) * PIECE)
-            quantize(z_words[:, cols], z_scales[:, cols], z[:])
+            quantize(z_words[:, cols], z_scales[:, cols], z[half][:])
             banks = product(
                 lambda t: w2_words[:, t * P : (t + 1) * P].bitcast(FP8X4),
                 lambda t: w2_scales[:, t * P : (t + 1) * P],
                 z_words[:, cols],
                 z_scales[:, cols],
             )
-            h_half = ring.tile([P, PACK, PIECE], F32, tag="h", name="h_half", align_bytes=64)
             for rows, bank in banks:
-                nc.scalar.copy(out=h_half[:, rows, :], in_=bank[:])
-            h.append(h_half)
+                nc.scalar.copy(out=h[half][:, rows, :], in_=bank[:])
+
+        for t in range(PACK):
+            line_up(0, t)
+        line_up(1, PACK - 1)
+        pool(0)
+        line_up(1, 0)
+        project(0)
+        for t in range(1, PACK - 1):
+            line_up(1, t)
+        pool(1)
+        project(1)
 
         for half in range(V // PIECE):
             for t in range(PACK):
                 nc.vector.tensor_copy(page[t][:].indirect(entries(n2_sb, half * PIECE, PIECE)), h[half][:, t, :])
 
-        fetches = [(0, 2 * PIECE), (2 * PIECE, PIECE), (3 * PIECE, PIECE)]
-        doubled = [held([P, PACK, width], F32, "doubled%d" % first) for first, width in fetches]
-        mixed = [held([P, PACK, width], F32, "mixed%d" % first) for first, width in fetches]
-        for f, (first, width) in enumerate(fetches):
-            for t in range(PACK):
-                nc.scalar.activation(doubled[f][:, t, :], page[t][:, first : first + width], COPY, scale=2.0)
-        for f, (first, width) in enumerate(fetches):
-            for t in range(PACK):
-                nc.vector.tensor_tensor(mixed[f][:, t, :], page[t][:].indirect(entries(n3_sb, first, width)), doubled[f][:, t, :], ALU.subtract)
+        fetches = U // PIECE
+        doubled = [held([P, PACK, PIECE], F32, "doubled%d" % f) for f in range(fetches)]
+        mixed = [held([P, PACK, PIECE], F32, "mixed%d" % f) for f in range(fetches)]
+
+        def mix(f, tiles):
+            for t in tiles:
+                nc.scalar.activation(doubled[f][:, t, :], page[t][:, f * PIECE : (f + 1) * PIECE], COPY, scale=2.0)
+            for t in tiles:
+                nc.vector.tensor_tensor(mixed[f][:, t, :], page[t][:].indirect(entries(n3_sb, f * PIECE, PIECE)), doubled[f][:, t, :], ALU.subtract)
 
         units = []
-        for f, (first, width) in enumerate(fetches):
-            step = PIECE if f < len(fetches) - 1 else PIECE // 2
-            for start in range(0, width, step):
-                units.append((slice(first + start, first + start + step), mixed[f][:, :, start : start + step]))
+        for f in range(fetches):
+            width = PIECE if f < fetches - 1 else PIECE // 2
+            for start in range(0, PIECE, width):
+                units.append((slice(f * PIECE + start, f * PIECE + start + width), mixed[f][:, :, start : start + width]))
 
         z2_words = held([P, U], U32, "z2_words")
         z2_scales = held([P, U], U8, "z2_scales")
@@ -240,10 +254,22 @@ def tile_picked_deeppoolpagem_none_po_kernel(
             quantize(out_words[:, cols], out_scales[:, cols], rounded[:])
             nc.sync.dma_start(out=out_1_words[:, cols], in_=out_words[:, cols].bitcast(I32))
 
-        for step in range(len(units) + 2):
-            for lag, stage in enumerate((multiply, add_residual, hand_on)):
-                if 0 <= step - lag < len(units):
-                    stage(step - lag)
+        last = len(units) - 1
+        mix(0, range(PACK))
+        for f in range(1, fetches):
+            mix(f, range(PACK // 2))
+            multiply(f - 1)
+            mix(f, range(PACK // 2, PACK))
+            if f >= 2:
+                hand_on(f - 2)
+            if f == fetches - 1:
+                multiply(last - 1)
+                multiply(last)
+            add_residual(f - 1)
+        hand_on(last - 2)
+        for stage in (add_residual, hand_on):
+            stage(last - 1)
+            stage(last)
         for quad in range(4):
             engine = nc.sync if quad % 2 else nc.scalar
             engine.dma_start(out=out_2[0][4 * quad : 4 * quad + 4, :].bitcast(I32), in_=out_scales[32 * quad : 32 * quad + 4, :].bitcast(I32))

@@ -33,8 +33,8 @@ def load_scale_rows(engine, tile, rows):
         engine.dma_start(out=tile[32 * quad : 32 * quad + 4, :].bitcast(I32), in_=rows[4 * quad : 4 * quad + 4, :].bitcast(I32))
 
 
-def woven(tile):
-    return tile.rearrange("p (c i t) -> p c t i", i=RUN, t=PACK)
+def woven(tile, run=RUN):
+    return tile.rearrange("p (c i t) -> p c t i", i=run, t=PACK)
 
 
 def planar(tile):
@@ -87,51 +87,54 @@ def tile_picked_deeppoolpagem_none_po_kernel(
             nc.sync.dma_start(out=page[t][:], in_=mem_rows[:, t, :])
         nc.sync.dma_start(out=res_sb[:], in_=res.rearrange("(p t) w -> p t w", t=PACK))
 
+        early = S - PIECE
         x_pick_scales = held([P, S], U8, "x_pick_scales")
-        x_pick_words = held([P, S], U32, "x_pick_words")
+        x_early_words = held([P, early], U32, "x_early_words")
         nc.vector.tensor_copy(x_pick_scales[:], x_scales_sb[:].indirect(offs_sb[:]))
-        nc.vector.tensor_copy(x_pick_words[:], x_words_sb[:].indirect(offs_sb[:]))
+        nc.vector.tensor_copy(x_early_words[:], x_words_sb[:].indirect(entries(offs_sb, 0, early)))
 
-        def deal_weight(dealt, raw, first_m):
+        def deal_weight(dealt, raw, first_m, first_t):
             count = raw.shape[2] // PACK
+            tiles = dealt.shape[1] // (P * PACK)
             nc.scalar.copy(
-                out=dealt[:].rearrange("p (t m j) -> p m j t", t=PACK, j=PACK)[:, first_m : first_m + count],
-                in_=raw.rearrange("p j (m t) -> p m j t", t=PACK),
+                out=dealt.rearrange("p (t m j) -> p m j t", t=tiles, j=PACK)[:, first_m : first_m + count],
+                in_=raw.rearrange("p j (m t) -> p m j t", t=PACK)[:, :, :, first_t : first_t + tiles],
             )
 
         def quantize(words, scales, values):
             nc.vector.quantize_mx(out=words.bitcast(FP8X4), scales=scales, in_=values)
 
-        w1_dealt = keep.tile([P, PACK * H], BF16, tag="dealt", name="w1_dealt", align_bytes=64)
+        w1_dealt = [keep.tile([P, 2 * H], BF16, tag="dealt%d" % pair, name="w1_dealt", align_bytes=64) for pair in range(2)]
         w1_words = held([P, H], U32, "w1_words")
         w1_scales = held([P, H], U8, "w1_scales")
         for c in range(2):
-            deal_weight(w1_dealt, w1_raw[c][:], c * (P // 2))
-        for c in range(2):
-            cols = slice(c * (H // 2), (c + 1) * (H // 2))
-            quantize(w1_words[:, cols], w1_scales[:, cols], w1_dealt[:, c * 2 * H : (c + 1) * 2 * H])
+            for pair in range(2):
+                deal_weight(w1_dealt[pair][:], w1_raw[c][:], c * (P // 2), 2 * pair)
+        quantize(w1_words[:, : H // 2], w1_scales[:, : H // 2], w1_dealt[0][:])
+        x_late_words = keep.tile([P, PIECE], U32, tag="dealt0", name="x_late_words", align_bytes=64)
+        nc.vector.tensor_copy(x_late_words[:], x_words_sb[:].indirect(entries(offs_sb, early, PIECE)))
+        quantize(w1_words[:, H // 2 :], w1_scales[:, H // 2 :], w1_dealt[1][:])
 
         y = [held([P, S], F32, "y%d" % t) for t in range(PACK)]
+        spans = [[(0, x_early_words[:, :BANK])], [(BANK, x_early_words[:, BANK:]), (early, x_late_words[:])]]
         for t in range(PACK):
             rows = slice(t * P, (t + 1) * P)
-            for half in range(S // BANK):
-                cols = slice(half * BANK, (half + 1) * BANK)
+            for half, parts in enumerate(spans):
                 bank = psum.tile([P, BANK], F32, tag="bank", name="y_bank")
-                nc.tensor.matmul_mx(
-                    out=bank[:],
-                    lhsT=w1_words[:, rows].bitcast(FP8X4),
-                    lhsT_scale=w1_scales[:, rows],
-                    rhs=x_pick_words[:, cols].bitcast(FP8X4),
-                    rhs_scale=x_pick_scales[:, cols],
-                    start=True,
-                    stop=True,
-                )
-                if t == 0 and half == 1:
-                    nc.vector.tensor_copy(out=y[t][:, cols], in_=bank[:])
-                else:
-                    nc.scalar.copy(out=y[t][:, cols], in_=bank[:])
+                for first, words in parts:
+                    width = words.shape[1]
+                    nc.tensor.matmul_mx(
+                        out=bank[:, first - half * BANK : first - half * BANK + width],
+                        lhsT=w1_words[:, rows].bitcast(FP8X4),
+                        lhsT_scale=w1_scales[:, rows],
+                        rhs=words.bitcast(FP8X4),
+                        rhs_scale=x_pick_scales[:, first : first + width],
+                        start=True,
+                        stop=True,
+                    )
+                nc.scalar.copy(out=y[t][:, half * BANK : (half + 1) * BANK], in_=bank[:])
 
-        w3_dealt_words = keep.tile([P, PACK, 2 * P], U8, tag="dealt", name="w3_dealt_words", align_bytes=64)
+        w3_dealt_words = keep.tile([P, PACK, 2 * P], U8, tag="dealt1", name="w3_dealt_words", align_bytes=64)
         w3_dealt_scales = held([P, PACK, P], U8, "w3_dealt_scales")
         nc.vector.tensor_copy(
             out=w3_dealt_words[:].rearrange("p t (m b) -> p t m b", b=2),
@@ -139,11 +142,13 @@ def tile_picked_deeppoolpagem_none_po_kernel(
         )
         nc.vector.tensor_copy(out=w3_dealt_scales[:], in_=w3_scales_sb[:].rearrange("p (m t) -> p t m", t=PACK))
 
-        w2_dealt = held([P, PACK * H], BF16, "w2_dealt")
+        slot = 2 * PIECE
+        lined = held([P, (PACK + 2) * slot], F32, "lined")
+        w2_dealt = lined[:, PACK * slot :].bitcast(BF16)
         w2_words = held([P, H], U32, "w2_words")
         w2_scales = held([P, H], U8, "w2_scales")
-        deal_weight(w2_dealt, w2_raw[:], 0)
-        quantize(w2_words[:], w2_scales[:], w2_dealt[:])
+        deal_weight(w2_dealt, w2_raw[:], 0, 0)
+        quantize(w2_words[:], w2_scales[:], w2_dealt)
 
         def product(lhs_words, lhs_scales, words, scales):
             width = words.shape[1]
@@ -162,16 +167,15 @@ def tile_picked_deeppoolpagem_none_po_kernel(
         z_words = held([P, V], U32, "z_words")
         z_scales = held([P, V], U8, "z_scales")
         halves = V // PIECE
-        lined = held([P, PACK + halves - 1, 2 * PIECE], F32, "lined")
         z = [held([P, PACK * PIECE], BF16, "z%d" % half) for half in range(halves)]
         h = [held([P, PACK, PIECE], F32, "h%d" % half) for half in range(halves)]
 
         def line_up(half, t):
-            nc.vector.tensor_copy(lined[:, half + t, :], y[t][:].indirect(entries(n1_sb, half * 2 * PIECE, 2 * PIECE)))
+            nc.vector.tensor_copy(lined[:, (2 * half + t) * slot : (2 * half + t + 1) * slot], y[t][:].indirect(entries(n1_sb, half * 2 * PIECE, 2 * PIECE)))
 
         def pool(half):
-            pairs = lined[:, half : half + PACK, :].rearrange("p t (c i e) -> p c t i e", i=RUN, e=2)
-            nc.vector.tensor_tensor(woven(z[half][:]), pairs[:, :, :, :, 0], pairs[:, :, :, :, 1], ALU.max)
+            pairs = lined[:, 2 * half * slot : (2 * half + PACK) * slot].rearrange("p (t c i e) -> p c t i e", t=PACK, i=RUN // 2, e=2)
+            nc.vector.tensor_tensor(woven(z[half][:], RUN // 2), pairs[:, :, :, :, 0], pairs[:, :, :, :, 1], ALU.max)
 
         def project(half):
             cols = slice(half * PIECE, (half + 1) * PIECE)
@@ -187,11 +191,10 @@ def tile_picked_deeppoolpagem_none_po_kernel(
 
         for t in range(PACK):
             line_up(0, t)
-        line_up(1, PACK - 1)
         pool(0)
         line_up(1, 0)
         project(0)
-        for t in range(1, PACK - 1):
+        for t in range(1, PACK):
             line_up(1, t)
         pool(1)
         project(1)
@@ -244,13 +247,16 @@ def tile_picked_deeppoolpagem_none_po_kernel(
                 nc.vector.tensor_tensor(results[u][:, rows, :], bank[:], res_sb[:, rows, cols], ALU.add)
             nc.sync.dma_start(out=out_rows[:, :, cols], in_=results[u][:])
 
-        def hand_on(u):
-            cols, source = units[u]
-            rounded = held([P, PACK * source.shape[2]], BF16, "rounded%d" % u)
-            if u == len(units) - 1:
-                nc.vector.tensor_copy(out=woven(rounded[:]), in_=planar(results[u][:]))
-            else:
-                nc.scalar.copy(out=woven(rounded[:]), in_=planar(results[u][:]))
+        def hand_on(*members):
+            cols = slice(units[members[0]][0].start, units[members[-1]][0].stop)
+            rounded = held([P, PACK * PIECE], BF16, "rounded%d" % members[0])
+            share = PACK * PIECE // len(members)
+            for i, u in enumerate(members):
+                part = woven(rounded[:, i * share : (i + 1) * share])
+                if u == len(units) - 1:
+                    nc.vector.tensor_copy(out=part, in_=planar(results[u][:]))
+                else:
+                    nc.scalar.copy(out=part, in_=planar(results[u][:]))
             quantize(out_words[:, cols], out_scales[:, cols], rounded[:])
             nc.sync.dma_start(out=out_1_words[:, cols], in_=out_words[:, cols].bitcast(I32))
 
@@ -267,9 +273,9 @@ def tile_picked_deeppoolpagem_none_po_kernel(
                 multiply(last)
             add_residual(f - 1)
         hand_on(last - 2)
-        for stage in (add_residual, hand_on):
-            stage(last - 1)
-            stage(last)
+        add_residual(last - 1)
+        add_residual(last)
+        hand_on(last - 1, last)
         for quad in range(4):
             engine = nc.sync if quad % 2 else nc.scalar
             engine.dma_start(out=out_2[0][4 * quad : 4 * quad + 4, :].bitcast(I32), in_=out_scales[32 * quad : 32 * quad + 4, :].bitcast(I32))

from contextlib import ExitStack

import concourse.mybir as mybir

K, T, S, V, N, H, U = 512, 2048, 1024, 512, 512, 512, 1024
FLOPS = 2 * K * H * S + 2 * H * H * V + 2 * H * N * U

F32 = mybir.dt.float32
BF16 = mybir.dt.bfloat16
I32 = mybir.dt.int32
U32 = mybir.dt.uint32
U16 = mybir.dt.uint16
U8 = mybir.dt.uint8
FP8X4 = mybir.dt.float8_e4m3fn_x4
FP4X4 = mybir.dt.float4_e2m1fn_x4
ALU = mybir.AluOpType
COPY = mybir.ActivationFunctionType.Copy

P = 128
PACK = 4
LIST_ROWS = 16
BANK = 512
PIECE = 256
RUN = 4


def entries(list_tile, first, count):
    return list_tile[:, first // LIST_ROWS : (first + count) // LIST_ROWS]


def load_scale_rows(engine, tile, rows):
    for quad in range(4):
        engine.dma_start(out=tile[32 * quad : 32 * quad + 4, :].bitcast(I32), in_=rows[4 * quad : 4 * quad + 4, :].bitcast(I32))


def woven(tile, run=RUN):
    return tile.rearrange("p (c i t) -> p c t i", i=run, t=PACK)


def planar(tile):
    return tile.rearrange("p t (c i) -> p c t i", i=RUN)


def tile_picked_deeppoolpagem_none_po_kernel(
    tc, x_words, x_scales, w1, w2, mem, w3_words, w3_scales, res, offs, n1, n2, n3, out_0, out_1, out_2
):
    nc = tc.nc
    with ExitStack() as ctx:
        keep = ctx.enter_context(tc.tile_pool(name="keep", bufs=1))
        ring = ctx.enter_context(tc.tile_pool(name="ring", bufs=2))
        psum = ctx.enter_context(tc.psum_pool(name="psum", bufs=8))

        def held(shape, dtype, name):
            return keep.tile(shape, dtype, name=name, align_bytes=64)

        offs_sb = held([P, S // LIST_ROWS], U16, "offs_sb")
        n1_sb = held([P, S // LIST_ROWS], U16, "n1_sb")
        n2_sb = held([P, V // LIST_ROWS], U16, "n2_sb")
        n3_sb = held([P, U // LIST_ROWS], U16, "n3_sb")
        x_words_sb = held([P, T], U32, "x_words_sb")
        x_scales_sb = held([P, T], U8, "x_scales_sb")
        w3_words_sb = held([P, 2 * N], U8, "w3_words_sb")
        w3_scales_sb = held([P, N], U8, "w3_scales_sb")
        w1_raw = [held([P, PACK, H // 2], F32, "w1_raw%d" % c) for c in range(2)]
        w2_raw = held([P, PACK, H], F32, "w2_raw")
        page = [held([P, U], F32, "page%d" % t) for t in range(PACK)]
        res_sb = held([P, PACK, U], F32, "res_sb")

        nc.vector.memset(x_scales_sb[:].bitcast(I32), 0)
        nc.gpsimd.memset(w3_scales_sb[:].bitcast(I32), 0)
        nc.sync.dma_start(offs_sb[:], offs)
        w1_rows = w1.rearrange("(p j) c -> p j c", j=PACK)
        nc.sync.dma_start(out=w1_raw[0][:], in_=w1_rows[:, :, : H // 2])
        load_scale_rows(nc.sync, x_scales_sb, x_scales[0])
        nc.sync.dma_start(out=x_words_sb[:].bitcast(I32), in_=x_words[0].rearrange("p n t -> p (n t)").bitcast(I32))
        nc.sync.dma_start(out=w1_raw[1][:], in_=w1_rows[:, :, H // 2 :])
        nc.sync.dma_start(out=w3_words_sb[:].bitcast(I32), in_=w3_words[0].bitcast(I32))
        load_scale_rows(nc.sync, w3_scales_sb, w3_scales[0])
        nc.sync.dma_start(n1_sb[:], n1)
        mem_rows = mem.rearrange("(p t) w -> p t w", t=PACK)
        for t in range(2):
            nc.sync.dma_start(out=page[t][:], in_=mem_rows[:, t, :])
        nc.sync.dma_start(out=w2_raw[:], in_=w2.rearrange("(p j) c -> p j c", j=PACK))
        nc.sync.dma_start(n2_sb[:], n2)
        nc.sync.dma_start(n3_sb[:], n3)
        for t in range(2, PACK):
            nc.sync.dma_start(out=page[t][:], in_=mem_rows[:, t, :])
        nc.sync.dma_start(out=res_sb[:], in_=res.rearrange("(p t) w -> p t w", t=PACK))

        early = S - PIECE
        x_pick_scales = held([P, S], U8, "x_pick_scales")
        x_early_words = held([P, early], U32, "x_early_words")
        nc.vector.tensor_copy(x_pick_scales[:], x_scales_sb[:].indirect(offs_sb[:]))
        nc.vector.tensor_copy(x_early_words[:], x_words_sb[:].indirect(entries(offs_sb, 0, early)))

        def deal_weight(dealt, raw, first_m, first_t):
            count = raw.shape[2] // PACK
            tiles = dealt.shape[1] // (P * PACK)
            nc.scalar.copy(
                out=dealt.rearrange("p (t m j) -> p m j t", t=tiles, j=PACK)[:, first_m : first_m + count],
                in_=raw.rearrange("p j (m t) -> p m j t", t=PACK)[:, :, :, first_t : first_t + tiles],
            )

        def quantize(words, scales, values):
            nc.vector.quantize_mx(out=words.bitcast(FP8X4), scales=scales, in_=values)

        w1_dealt = [keep.tile([P, 2 * H], BF16, tag="dealt%d" % pair, name="w1_dealt", align_bytes=64) for pair in range(2)]
        w1_words = held([P, H], U32, "w1_words")
        w1_scales = held([P, H], U8, "w1_scales")
        for c in range(2):
            for pair in range(2):
                deal_weight(w1_dealt[pair][:], w1_raw[c][:], c * (P // 2), 2 * pair)
        quantize(w1_words[:, : H // 2], w1_scales[:, : H // 2], w1_dealt[0][:])
        x_late_words = keep.tile([P, PIECE], U32, tag="dealt0", name="x_late_words", align_bytes=64)
        nc.vector.tensor_copy(x_late_words[:], x_words_sb[:].indirect(entries(offs_sb, early, PIECE)))
        quantize(w1_words[:, H // 2 :], w1_scales[:, H // 2 :], w1_dealt[1][:])

        y = [held([P, S], F32, "y%d" % t) for t in range(PACK)]
        spans = [[(0, x_early_words[:, :BANK])], [(BANK, x_early_words[:, BANK:]), (early, x_late_words[:])]]
        for t in range(PACK):
            rows = slice(t * P, (t + 1) * P)
            for half, parts in enumerate(spans):
                bank = psum.tile([P, BANK], F32, tag="bank", name="y_bank")
                for first, words in parts:
                    width = words.shape[1]
                    nc.tensor.matmul_mx(
                        out=bank[:, first - half * BANK : first - half * BANK + width],
                        lhsT=w1_words[:, rows].bitcast(FP8X4),
                        lhsT_scale=w1_scales[:, rows],
                        rhs=words.bitcast(FP8X4),
                        rhs_scale=x_pick_scales[:, first : first + width],
                        start=True,
                        stop=True,
                    )
                nc.scalar.copy(out=y[t][:, half * BANK : (half + 1) * BANK], in_=bank[:])

        w3_dealt_words = keep.tile([P, PACK, 2 * P], U8, tag="dealt1", name="w3_dealt_words", align_bytes=64)
        w3_dealt_scales = held([P, PACK, P], U8, "w3_dealt_scales")
        nc.vector.tensor_copy(
            out=w3_dealt_words[:].rearrange("p t (m b) -> p t m b", b=2),
            in_=w3_words_sb[:].rearrange("p (m t b) -> p t m b", t=PACK, b=2),
        )
        nc.vector.tensor_copy(out=w3_dealt_scales[:], in_=w3_scales_sb[:].rearrange("p (m t) -> p t m", t=PACK))

        slot = 2 * PIECE
        lined = held([P, (PACK + 2) * slot], F32, "lined")
        w2_dealt = lined[:, PACK * slot :].bitcast(BF16)
        w2_words = held([P, H], U32, "w2_words")
        w2_scales = held([P, H], U8, "w2_scales")
        deal_weight(w2_dealt, w2_raw[:], 0, 0)
        quantize(w2_words[:], w2_scales[:], w2_dealt)

        def product(lhs_words, lhs_scales, words, scales):
            width = words.shape[1]
            share = BANK // width
            banks = []
            for first in range(0, PACK, share):
                bank = psum.tile([P, share, width], F32, tag="bank", name="shared_bank")
                for i in range(share):
                    t = first + i
                    nc.tensor.matmul_mx(
                        out=bank[:, i, :], lhsT=lhs_words(t), lhsT_scale=lhs_scales(t), rhs=words.bitcast(FP8X4), rhs_scale=scales, start=True, stop=True
                    )
                banks.append((slice(first, first + share), bank))
            return banks

        z_words = held([P, V], U32, "z_words")
        z_scales = held([P, V], U8, "z_scales")
        halves = V // PIECE
        z = [held([P, PACK * PIECE], BF16, "z%d" % half) for half in range(halves)]
        h = [held([P, PACK, PIECE], F32, "h%d" % half) for half in range(halves)]

        def line_up(half, t):
            nc.vector.tensor_copy(lined[:, (2 * half + t) * slot : (2 * half + t + 1) * slot], y[t][:].indirect(entries(n1_sb, half * 2 * PIECE, 2 * PIECE)))

        def pool(half):
            pairs = lined[:, 2 * half * slot : (2 * half + PACK) * slot].rearrange("p (t c i e) -> p c t i e", t=PACK, i=RUN // 2, e=2)
            nc.vector.tensor_tensor(woven(z[half][:], RUN // 2), pairs[:, :, :, :, 0], pairs[:, :, :, :, 1], ALU.max)

        def project(half):
            cols = slice(half * PIECE, (half + 1) * PIECE)
            quantize(z_words[:, cols], z_scales[:, cols], z[half][:])
            banks = product(
                lambda t: w2_words[:, t * P : (t + 1) * P].bitcast(FP8X4),
                lambda t: w2_scales[:, t * P : (t + 1) * P],
                z_words[:, cols],
                z_scales[:, cols],
            )
            for rows, bank in banks:
                nc.scalar.copy(out=h[half][:, rows, :], in_=bank[:])

        for t in range(PACK):
            line_up(0, t)
        pool(0)
        line_up(1, 0)
        project(0)
        for t in range(1, PACK):
            line_up(1, t)
        pool(1)
        project(1)

        for half in range(V // PIECE):
            for t in range(PACK):
                nc.vector.tensor_copy(page[t][:].indirect(entries(n2_sb, half * PIECE, PIECE)), h[half][:, t, :])

        fetches = U // PIECE
        doubled = [held([P, PACK, PIECE], F32, "doubled%d" % f) for f in range(fetches)]
        mixed = [held([P, PACK, PIECE], F32, "mixed%d" % f) for f in range(fetches)]

        def mix(f, tiles):
            for t in tiles:
                nc.scalar.activation(doubled[f][:, t, :], page[t][:, f * PIECE : (f + 1) * PIECE], COPY, scale=2.0)
            for t in tiles:
                nc.vector.tensor_tensor(mixed[f][:, t, :], page[t][:].indirect(entries(n3_sb, f * PIECE, PIECE)), doubled[f][:, t, :], ALU.subtract)

        units = []
        for f in range(fetches):
            width = PIECE if f < fetches - 1 else PIECE // 2
            for start in range(0, PIECE, width):
                units.append((slice(f * PIECE + start, f * PIECE + start + width), mixed[f][:, :, start : start + width]))

        z2_words = held([P, U], U32, "z2_words")
        z2_scales = held([P, U], U8, "z2_scales")
        out_words = held([P, U], U32, "out_words")
        out_scales = held([P, U], U8, "out_scales")
        out_rows = out_0.rearrange("(p t) w -> p t w", t=PACK)
        out_1_words = out_1[0].rearrange("p n t -> p (n t)").bitcast(I32)
        sums = {}
        results = {}

        def multiply(u):
            cols, source = units[u]
            z2 = held([P, PACK * source.shape[2]], BF16, "z2_%d" % u)
            nc.scalar.activation(woven(z2[:]), planar(source), COPY, scale=-0.5)
            quantize(z2_words[:, cols], z2_scales[:, cols], z2[:])
            sums[u] = product(
                lambda t: w3_dealt_words[:, t, :].bitcast(FP4X4),
                lambda t: w3_dealt_scales[:, t, :],
                z2_words[:, cols],
                z2_scales[:, cols],
            )

        def add_residual(u):
            cols, source = units[u]
            results[u] = held([P, PACK, source.shape[2]], F32, "result%d" % u)
            for rows, bank in sums[u]:
                nc.vector.tensor_tensor(results[u][:, rows, :], bank[:], res_sb[:, rows, cols], ALU.add)
            nc.sync.dma_start(out=out_rows[:, :, cols], in_=results[u][:])

        def hand_on(*members):
            cols = slice(units[members[0]][0].start, units[members[-1]][0].stop)
            rounded = held([P, PACK * PIECE], BF16, "rounded%d" % members[0])
            share = PACK * PIECE // len(members)
            for i, u in enumerate(members):
                part = woven(rounded[:, i * share : (i + 1) * share])
                if u == len(units) - 1:
                    nc.vector.tensor_copy(out=part, in_=planar(results[u][:]))
                else:
                    nc.scalar.copy(out=part, in_=planar(results[u][:]))
            quantize(out_words[:, cols], out_scales[:, cols], rounded[:])
            nc.sync.dma_start(out=out_1_words[:, cols], in_=out_words[:, cols].bitcast(I32))

        last = len(units) - 1
        mix(0, range(PACK))
        for f in range(1, fetches):
            mix(f, range(PACK // 2))
            multiply(f - 1)
            mix(f, range(PACK // 2, PACK))
            if f >= 2:
                hand_on(f - 2)
            if f == fetches - 1:
                multiply(last - 1)
                multiply(last)
            add_residual(f - 1)
        hand_on(last - 2)
        add_residual(last - 1)
        add_residual(last)
        hand_on(last - 1, last)
        for quad in range(4):
            engine = nc.sync if quad % 2 else nc.scalar
            engine.dma_start(out=out_2[0][4 * quad : 4 * quad + 4, :].bitcast(I32), in_=out_scales[32 * quad : 32 * quad + 4, :].bitcast(I32))
